import numpy as np, ml_dtypes
CORES = [61,69,101,62,70,102]
N = 6
import mx_ref
NC, G = 128, 4
C = np.float32(0.041)
BF = ml_dtypes.bfloat16
def cut(t, i, w=512):
    return t[:, w * i:w * i + w]
def tile(rs):
    return np.stack(rs, axis=2).reshape(128, -1).astype(BF)
def layer(w, X):
    out = []
    for i in range(G):
        for t in range(len(X)):
            p = mx_ref.matmul(mx_ref.quantize(cut(w, len(X) * i + t)), X[t])
            z = p if t == 0 else z + p
        out.append(z)
    return out
def act(Z):
    return [np.maximum(z, 0) * C for z in Z]
def setup_inputs(rng):
    def f(*shape):
        return mx_ref.flush((rng.standard_normal(shape, dtype=np.float32) * np.exp2(rng.integers(-2, 3, shape[:-1] + (1,)))).astype(BF))
    return {"x": f(N, 128, 4 * NC), "w1": f(N, 128, G * 512), "w2": f(N, 128, 512)}
def setup_inputs_blocks(rng):
    d = setup_inputs(rng)
    for k in ("x", "w1", "w2"): d[k] = mx_ref.spread(d[k], rng, 4)
    return d
def setup_inputs_wide(rng):
    d = setup_inputs(rng)
    for k in ("x", "w1", "w2"): d[k] = mx_ref.flush((d[k].astype(np.float32) * np.exp2(rng.integers(-8, 9, (N, 1, 1))).astype(np.float32)).astype(BF))
    return d
def setup_inputs_zeros(rng):
    d = setup_inputs(rng); v = d["x"].reshape(N, 128, -1, 4).copy()
    v[np.broadcast_to((rng.random((N, 1, v.shape[2], 1)) < 0.33), v.shape)] = 0
    d["x"] = v.reshape(d["x"].shape)
    return d
def reference(x, w1, w2):
    H = [mx_ref.quantize(tile(act(layer(w1[j], [mx_ref.quantize(x[j])])))) for j in range(N)]
    y = np.full((N, 128, N * NC), np.nan, np.float32)
    for r in range(N):
        qw = mx_ref.quantize(w2[r])
        for j in range(r + 1):
            y[r][:, NC * j:NC * j + NC] = mx_ref.matmul(qw, H[j])
    return {"y": y}

@@ -1,0 +1,182 @@
+from concourse.bass import DstId, RemoteDMATransfer
+from concourse.mybir import dt, AluOpType, ActivationFunctionType
+
+N = 6
+NC = 128
+G = 4
+C = 0.041
+BANK = 512
+
+GATE_ENGINES = 8
+PASS_GROUPS = 1
+
+SCRATCH = {
+    "xb": ("sbuf", [128, 4 * NC], "bfloat16"),
+    "w1b": ("sbuf", [128, G * 512], "bfloat16"),
+    "w2b": ("sbuf", [128, 512], "bfloat16"),
+    "hb": ("sbuf", [128, 4 * NC], "bfloat16"),
+    "xq": ("sbuf", [128, NC], "float8_e4m3fn_x4"),
+    "xs": ("sbuf", [128, NC], "uint8"),
+    "w1q": ("sbuf", [128, G * 128], "float8_e4m3fn_x4"),
+    "w1s": ("sbuf", [128, G * 128], "uint8"),
+    "w2q": ("sbuf", [128, 128], "float8_e4m3fn_x4"),
+    "w2s": ("sbuf", [128, 128], "uint8"),
+    "hq": ("sbuf", [128, N * NC], "float8_e4m3fn_x4"),
+    "hs": ("sbuf", [128, N * NC], "uint8"),
+    "yb": ("sbuf", [128, N * NC], "float32"),
+    "ps": ("psum", [128, 8 * BANK], "float32"),
+}
+SEMAPHORES = (["lx", "lwa", "lwb", "lv", "qx", "qh", "qv", "acs", "acv", "sent"]
+              + ["qw%d" % i for i in range(G)] + ["m%d" % i for i in range(G)]
+              + ["c%d" % j for j in range(N)] + ["s%d" % j for j in range(N)]
+              + ["y%d" % k for k in range(N)] + ["cp%d" % k for k in range(N)] + ["st%d" % k for k in range(N)])
+
+
+def _plan(cores, topo):
+    stage0, stage1, stage2 = [], [], []
+    last_chip = topo.chip(cores[-1])
+    for j, s in enumerate(cores):
+        need = cores[j + 1:]
+        reach = [d for d in need if topo.may_write(s, d)]
+        rest = [d for d in need if not topo.may_write(s, d)]
+        gate = None
+        if rest:
+            gate = [c for c in reach if all(topo.may_write(c, d) for d in rest)][0]
+            stage0.append([0, s, j, j + 1, [gate], GATE_ENGINES])
+        away = [d for d in reach if d != gate and topo.chip(d) != topo.chip(s)]
+        home = [d for d in reach if d != gate and topo.chip(d) == topo.chip(s)]
+        if away:
+            stage0.append([0, s, j, j + 1, away, 16])
+        if home:
+            stage0.append([0, s, j, j + 1, home, 16])
+        if rest:
+            chips = []
+            for d in rest:
+                if topo.chip(d) not in chips:
+                    chips.append(topo.chip(d))
+            chips.sort(key=lambda ch: (ch != last_chip, -ch))
+            handed = 0
+            for ch in chips:
+                grp = [d for d in rest if topo.chip(d) == ch]
+                if len(grp) > 1 and handed < PASS_GROUPS:
+                    handed += 1
+                    stage1.append([1, gate, j, j + 1, grp[:1], 16])
+                    stage2.append([2, grp[0], j, j + 1, grp[1:], 16])
+                else:
+                    stage1.append([1, gate, j, j + 1, grp, 16])
+    merged = []
+    for h in stage1:
+        if merged and merged[-1][1] == h[1] and merged[-1][4] == h[4] and merged[-1][3] == h[2]:
+            merged[-1][3] = h[3]
+        else:
+            merged.append(h)
+    return stage0 + merged + stage2
+
+
+def _mask(topo, src, dsts, k):
+    m = topo.mask(src, dsts[0])
+    for d in dsts[1:]:
+        m &= topo.mask(src, d)
+    bits = [b for b in range(m.bit_length()) if (m >> b) & 1][:k]
+    return sum(1 << b for b in bits), len(bits)
+
+
+def rank_program(g, core, T, topo):
+    cores = [int(c) for c in T.cores]
+    S = T.sem
+    hops = _plan(cores, topo)
+    mine = [h for h in hops if h[1] == core]
+    inbound = [h for h in hops if core in h[4]]
+    rank = T.rank_of(core)
+    if rank is None and not mine and not inbound:
+        return
+
+    def cols(t, lo, hi):
+        return t[:, NC * lo:NC * hi]
+
+    def here(t, kind):
+        if rank is not None and t == rank:
+            return ("qh", 1)
+        for (_, src, lo, hi, dsts, k) in inbound:
+            if lo <= t < hi:
+                return ("%s%d" % (kind, lo), _mask(topo, src, dsts, k)[1])
+        return None
+
+    stores = 0
+    if rank is not None:
+        v, pe, sc, sy = g.vector, g.tensor, g.scalar, g.sync
+        a = (G - 1) * 512
+        sy.dma_start(T.xb[:], T.x[:]).then_inc(S.lx, 16)
+        sc.dma_start(T.w1b[:, 0:a], T.w1[:, 0:a]).then_inc(S.lwa, 16)
+        sy.dma_start(T.w1b[:, a:a + 512], T.w1[:, a:a + 512]).then_inc(S.lwb, 16)
+        sy.dma_start(T.w2b[:], T.w2[:]).then_inc(S.lv, 16)
+
+        v.wait_ge(S.lx, 16)
+        v.quantize_mx(T.xq[:], T.xs[:], T.xb[:]).then_inc(S.qx, 1)
+        pe.wait_ge(S.qx, 1)
+        for i in range(G):
+            if i == 0:
+                v.wait_ge(S.lwa, 16)
+            if i == G - 1:
+                v.wait_ge(S.lwb, 16)
+            v.quantize_mx(T.w1q[:, 128 * i:128 * i + 128], T.w1s[:, 128 * i:128 * i + 128],
+                          T.w1b[:, 512 * i:512 * i + 512]).then_inc(S["qw%d" % i], 1)
+            pe.wait_ge(S["qw%d" % i], 1)
+            pe.matmul_mx(T.ps[:, BANK * i:BANK * i + NC], T.w1q[:, 128 * i:128 * i + 128],
+                         T.w1s[:, 128 * i:128 * i + 128], T.xq[:], T.xs[:], True, True).then_inc(S["m%d" % i], 1)
+        for i in range(G - 1):
+            sc.wait_ge(S["m%d" % i], 1)
+            sc.activation(T.hb[:, i:4 * NC:4], T.ps[:, BANK * i:BANK * i + NC], ActivationFunctionType.Relu,
+                          scale=C).then_inc(S.acs, 1)
+        i = G - 1
+        v.wait_ge(S["m%d" % i], 1)
+        v.tensor_scalar(T.hb[:, i:4 * NC:4], T.ps[:, BANK * i:BANK * i + NC], 0.0, C,
+                        AluOpType.max, AluOpType.mult).then_inc(S.acv, 1)
+        v.wait_ge(S.acs, G - 1)
+        v.wait_ge(S.acv, 1)
+        v.quantize_mx(cols(T.hq, rank, rank + 1), cols(T.hs, rank, rank + 1), T.hb[:]).then_inc(S.qh, 1)
+        v.wait_ge(S.lv, 16)
+        v.quantize_mx(T.w2q[:], T.w2s[:], T.w2b[:]).then_inc(S.qv, 1)
+
+        order = sorted(inbound, key=lambda h: (h[0], [x for x in hops if x[1] == h[1]].index(h), hops.index(h)))
+        units = [(rank, rank + 1)] + [(h[2], h[3]) for h in order]
+        pe.wait_ge(S.qv, 1)
+        for k, (lo, hi) in enumerate(units):
+            for w in sorted(set(here(t, kind) for t in range(lo, hi) for kind in "cs")):
+                pe.wait_ge(S[w[0]], w[1])
+            if k >= 4:
+                pe.wait_ge(S["cp%d" % (k - 4)], 1)
+            b = BANK * (4 + k % 4)
+            z = T.ps[:, b:b + NC * (hi - lo)]
+            pe.matmul_mx(z, T.w2q[:], T.w2s[:], cols(T.hq, lo, hi), cols(T.hs, lo, hi), True, True).then_inc(S["y%d" % k], 1)
+            v.wait_ge(S["y%d" % k], 1)
+            v.tensor_copy(cols(T.yb, lo, hi), z).then_inc(S["cp%d" % k], 1)
+            sy.wait_ge(S["cp%d" % k], 1)
+            sy.dma_start(cols(T.y, lo, hi), cols(T.yb, lo, hi)).then_inc(S["st%d" % k], 16)
+        stores = len(units)
+
+    sent = 0
+    waited = []
+    for (_, src, lo, hi, dsts, k) in mine:
+        mask, n = _mask(topo, core, dsts, k)
+        for kind in "cs":
+            for t in range(lo, hi):
+                w = here(t, kind)
+                if w not in waited:
+                    waited.append(w)
+                    g.wait_ge(S[w[0]], w[1])
+            view = cols(T.hq, lo, hi).bitcast(dt.uint8) if kind == "c" else cols(T.hs, lo, hi)
+            sem = S["%s%d" % (kind, lo)]
+            ids = [topo.addr(d) for d in dsts]
+            if len(dsts) == 1:
+                g.remote_dma(out_ap=view, in_ap=view, remote_sem=sem, local_sem=S.sent, pid=ids[0][1],
+                             routing_id=ids[0][0], dma_engine_mask=mask)
+            else:
+                g.remote_dma_fused([RemoteDMATransfer(dst_ids=[DstId(rid=r, pnc=p) for (r, p, _) in ids],
+                                                      dma_engine_mask=mask, remote_sem=sem, srcs=[view],
+                                                      dsts=[view for _ in dsts])], local_sem=S.sent)
+            sent += n
+    if sent:
+        g.wait_ge(S.sent, sent)
+    for k in range(stores):
+        g.wait_ge(S["st%d" % k], 16)

@@ -6,9 +6,7 @@ NC = 128
 G = 4
 C = 0.041
 BANK = 512
-
-GATE_ENGINES = 8
-PASS_GROUPS = 1
+SPLIT = (3, 1)
 
 SCRATCH = {
     "xb": ("sbuf", [128, 4 * NC], "bfloat16"),
@@ -26,59 +24,65 @@ SCRATCH = {
     "yb": ("sbuf", [128, N * NC], "float32"),
     "ps": ("psum", [128, 8 * BANK], "float32"),
 }
-SEMAPHORES = (["lx", "lwa", "lwb", "lv", "qx", "qh", "qv", "acs", "acv", "sent"]
-              + ["qw%d" % i for i in range(G)] + ["m%d" % i for i in range(G)]
+SEMAPHORES = (["lx", "lv", "qx", "qh", "qv", "acs", "acv", "sent"]
+              + ["lw%d" % i for i in range(G)] + ["qw%d" % i for i in range(G)] + ["m%d" % i for i in range(G)]
               + ["c%d" % j for j in range(N)] + ["s%d" % j for j in range(N)]
               + ["y%d" % k for k in range(N)] + ["cp%d" % k for k in range(N)] + ["st%d" % k for k in range(N)])
 
 
 def _plan(cores, topo):
-    stage0, stage1, stage2 = [], [], []
+    hops = []
     last_chip = topo.chip(cores[-1])
+
+    def chips_of(dsts):
+        chips = []
+        for d in dsts:
+            if topo.chip(d) not in chips:
+                chips.append(topo.chip(d))
+        return sorted(chips, key=lambda ch: (ch != last_chip, -ch))
+
+    def deliver(stage, via, j, dsts):
+        for ch in chips_of(dsts):
+            grp = [d for d in dsts if topo.chip(d) == ch]
+            if ch != topo.chip(via) and len(grp) > 1:
+                hops.append([stage, via, j, grp[:1]])
+                hops.append([stage + 1, grp[0], j, grp[1:]])
+            else:
+                hops.append([stage, via, j, grp])
+
+    gates, busy = {}, []
     for j, s in enumerate(cores):
-        need = cores[j + 1:]
-        reach = [d for d in need if topo.may_write(s, d)]
-        rest = [d for d in need if not topo.may_write(s, d)]
-        gate = None
+        reach = [d for d in cores[j + 1:] if topo.may_write(s, d)]
+        rest = [d for d in cores[j + 1:] if not topo.may_write(s, d)]
         if rest:
-            gate = [c for c in reach if all(topo.may_write(c, d) for d in rest)][0]
-            stage0.append([0, s, j, j + 1, [gate], GATE_ENGINES])
+            gates[j] = [c for c in reach if all(topo.may_write(c, d) for d in rest)][0]
+            if len(chips_of(rest)) > 1:
+                busy.append(gates[j])
+    for j, s in enumerate(cores):
+        reach = [d for d in cores[j + 1:] if topo.may_write(s, d)]
+        rest = [d for d in cores[j + 1:] if not topo.may_write(s, d)]
+        gate = gates.get(j)
+        if rest:
+            hops.append([0, s, j, [gate]])
         away = [d for d in reach if d != gate and topo.chip(d) != topo.chip(s)]
         home = [d for d in reach if d != gate and topo.chip(d) == topo.chip(s)]
-        if away:
-            stage0.append([0, s, j, j + 1, away, 16])
+        if s in busy and len(away) > 1:
+            deliver(0, s, j, away[:1])
+            deliver(3, s, j, away[1:])
+        elif away:
+            deliver(0, s, j, away)
         if home:
-            stage0.append([0, s, j, j + 1, home, 16])
+            hops.append([0, s, j, home])
         if rest:
-            chips = []
-            for d in rest:
-                if topo.chip(d) not in chips:
-                    chips.append(topo.chip(d))
-            chips.sort(key=lambda ch: (ch != last_chip, -ch))
-            handed = 0
-            for ch in chips:
-                grp = [d for d in rest if topo.chip(d) == ch]
-                if len(grp) > 1 and handed < PASS_GROUPS:
-                    handed += 1
-                    stage1.append([1, gate, j, j + 1, grp[:1], 16])
-                    stage2.append([2, grp[0], j, j + 1, grp[1:], 16])
-                else:
-                    stage1.append([1, gate, j, j + 1, grp, 16])
-    merged = []
-    for h in stage1:
-        if merged and merged[-1][1] == h[1] and merged[-1][4] == h[4] and merged[-1][3] == h[2]:
-            merged[-1][3] = h[3]
-        else:
-            merged.append(h)
-    return stage0 + merged + stage2
+            deliver(1, gate, j, rest)
+    return sorted(hops, key=lambda h: h[0])
 
 
-def _mask(topo, src, dsts, k):
+def _mask(topo, src, dsts):
     m = topo.mask(src, dsts[0])
     for d in dsts[1:]:
         m &= topo.mask(src, d)
-    bits = [b for b in range(m.bit_length()) if (m >> b) & 1][:k]
-    return sum(1 << b for b in bits), len(bits)
+    return m, sum((m >> b) & 1 for b in range(m.bit_length()))
 
 
 def rank_program(g, core, T, topo):
@@ -86,39 +90,41 @@ def rank_program(g, core, T, topo):
     S = T.sem
     hops = _plan(cores, topo)
     mine = [h for h in hops if h[1] == core]
-    inbound = [h for h in hops if core in h[4]]
+    inbound = [h for h in hops if core in h[3]]
     rank = T.rank_of(core)
     if rank is None and not mine and not inbound:
         return
 
-    def cols(t, lo, hi):
-        return t[:, NC * lo:NC * hi]
+    def cols(t, j):
+        return t[:, NC * j:NC * j + NC]
 
     def here(t, kind):
         if rank is not None and t == rank:
             return ("qh", 1)
-        for (_, src, lo, hi, dsts, k) in inbound:
-            if lo <= t < hi:
-                return ("%s%d" % (kind, lo), _mask(topo, src, dsts, k)[1])
+        for (_, src, j, dsts) in inbound:
+            if j == t:
+                return ("%s%d" % (kind, j), _mask(topo, src, dsts)[1])
         return None
 
     stores = 0
     if rank is not None:
         v, pe, sc, sy = g.vector, g.tensor, g.scalar, g.sync
-        a = (G - 1) * 512
         sy.dma_start(T.xb[:], T.x[:]).then_inc(S.lx, 16)
-        sc.dma_start(T.w1b[:, 0:a], T.w1[:, 0:a]).then_inc(S.lwa, 16)
-        sy.dma_start(T.w1b[:, a:a + 512], T.w1[:, a:a + 512]).then_inc(S.lwb, 16)
+        first = {}
+        t0 = 0
+        for n, w in enumerate(SPLIT):
+            q = sc if n % 2 == 0 else sy
+            q.dma_start(T.w1b[:, 512 * t0:512 * (t0 + w)], T.w1[:, 512 * t0:512 * (t0 + w)]).then_inc(S["lw%d" % n], 16)
+            first[t0] = "lw%d" % n
+            t0 += w
         sy.dma_start(T.w2b[:], T.w2[:]).then_inc(S.lv, 16)
 
         v.wait_ge(S.lx, 16)
         v.quantize_mx(T.xq[:], T.xs[:], T.xb[:]).then_inc(S.qx, 1)
         pe.wait_ge(S.qx, 1)
         for i in range(G):
-            if i == 0:
-                v.wait_ge(S.lwa, 16)
-            if i == G - 1:
-                v.wait_ge(S.lwb, 16)
+            if i in first:
+                v.wait_ge(S[first[i]], 16)
             v.quantize_mx(T.w1q[:, 128 * i:128 * i + 128], T.w1s[:, 128 * i:128 * i + 128],
                           T.w1b[:, 512 * i:512 * i + 512]).then_inc(S["qw%d" % i], 1)
             pe.wait_ge(S["qw%d" % i], 1)
@@ -134,39 +140,38 @@ def rank_program(g, core, T, topo):
                         AluOpType.max, AluOpType.mult).then_inc(S.acv, 1)
         v.wait_ge(S.acs, G - 1)
         v.wait_ge(S.acv, 1)
-        v.quantize_mx(cols(T.hq, rank, rank + 1), cols(T.hs, rank, rank + 1), T.hb[:]).then_inc(S.qh, 1)
+        v.quantize_mx(cols(T.hq, rank), cols(T.hs, rank), T.hb[:]).then_inc(S.qh, 1)
         v.wait_ge(S.lv, 16)
         v.quantize_mx(T.w2q[:], T.w2s[:], T.w2b[:]).then_inc(S.qv, 1)
 
         order = sorted(inbound, key=lambda h: (h[0], [x for x in hops if x[1] == h[1]].index(h), hops.index(h)))
-        units = [(rank, rank + 1)] + [(h[2], h[3]) for h in order]
+        units = [rank] + [h[2] for h in order]
         pe.wait_ge(S.qv, 1)
-        for k, (lo, hi) in enumerate(units):
-            for w in sorted(set(here(t, kind) for t in range(lo, hi) for kind in "cs")):
+        for k, j in enumerate(units):
+            for w in sorted(set(here(j, kind) for kind in "cs")):
                 pe.wait_ge(S[w[0]], w[1])
             if k >= 4:
                 pe.wait_ge(S["cp%d" % (k - 4)], 1)
             b = BANK * (4 + k % 4)
-            z = T.ps[:, b:b + NC * (hi - lo)]
-            pe.matmul_mx(z, T.w2q[:], T.w2s[:], cols(T.hq, lo, hi), cols(T.hs, lo, hi), True, True).then_inc(S["y%d" % k], 1)
+            z = T.ps[:, b:b + NC]
+            pe.matmul_mx(z, T.w2q[:], T.w2s[:], cols(T.hq, j), cols(T.hs, j), True, True).then_inc(S["y%d" % k], 1)
             v.wait_ge(S["y%d" % k], 1)
-            v.tensor_copy(cols(T.yb, lo, hi), z).then_inc(S["cp%d" % k], 1)
+            v.tensor_copy(cols(T.yb, j), z).then_inc(S["cp%d" % k], 1)
             sy.wait_ge(S["cp%d" % k], 1)
-            sy.dma_start(cols(T.y, lo, hi), cols(T.yb, lo, hi)).then_inc(S["st%d" % k], 16)
+            sy.dma_start(cols(T.y, j), cols(T.yb, j)).then_inc(S["st%d" % k], 16)
         stores = len(units)
 
     sent = 0
     waited = []
-    for (_, src, lo, hi, dsts, k) in mine:
-        mask, n = _mask(topo, core, dsts, k)
+    for (_, src, j, dsts) in mine:
+        mask, n = _mask(topo, core, dsts)
         for kind in "cs":
-            for t in range(lo, hi):
-                w = here(t, kind)
-                if w not in waited:
-                    waited.append(w)
-                    g.wait_ge(S[w[0]], w[1])
-            view = cols(T.hq, lo, hi).bitcast(dt.uint8) if kind == "c" else cols(T.hs, lo, hi)
-            sem = S["%s%d" % (kind, lo)]
+            w = here(j, kind)
+            if w not in waited:
+                waited.append(w)
+                g.wait_ge(S[w[0]], w[1])
+            view = cols(T.hq, j).bitcast(dt.uint8) if kind == "c" else cols(T.hs, j)
+            sem = S["%s%d" % (kind, j)]
             ids = [topo.addr(d) for d in dsts]
             if len(dsts) == 1:
                 g.remote_dma(out_ap=view, in_ap=view, remote_sem=sem, local_sem=S.sent, pid=ids[0][1],

from concourse.bass import DstId, RemoteDMATransfer
from concourse.mybir import dt, AluOpType, ActivationFunctionType

N = 6
NC = 128
G = 4
C = 0.041
BANK = 512
SPLIT = (3, 1)

SCRATCH = {
    "xb": ("sbuf", [128, 4 * NC], "bfloat16"),
    "w1b": ("sbuf", [128, G * 512], "bfloat16"),
    "w2b": ("sbuf", [128, 512], "bfloat16"),
    "hb": ("sbuf", [128, 4 * NC], "bfloat16"),
    "xq": ("sbuf", [128, NC], "float8_e4m3fn_x4"),
    "xs": ("sbuf", [128, NC], "uint8"),
    "w1q": ("sbuf", [128, G * 128], "float8_e4m3fn_x4"),
    "w1s": ("sbuf", [128, G * 128], "uint8"),
    "w2q": ("sbuf", [128, 128], "float8_e4m3fn_x4"),
    "w2s": ("sbuf", [128, 128], "uint8"),
    "hq": ("sbuf", [128, N * NC], "float8_e4m3fn_x4"),
    "hs": ("sbuf", [128, N * NC], "uint8"),
    "yb": ("sbuf", [128, N * NC], "float32"),
    "ps": ("psum", [128, 8 * BANK], "float32"),
}
SEMAPHORES = (["lx", "lv", "qx", "qh", "qv", "acs", "acv", "sent"]
              + ["lw%d" % i for i in range(G)] + ["qw%d" % i for i in range(G)] + ["m%d" % i for i in range(G)]
              + ["c%d" % j for j in range(N)] + ["s%d" % j for j in range(N)]
              + ["y%d" % k for k in range(N)] + ["cp%d" % k for k in range(N)] + ["st%d" % k for k in range(N)])


def _plan(cores, topo):
    hops = []
    last_chip = topo.chip(cores[-1])

    def chips_of(dsts):
        chips = []
        for d in dsts:
            if topo.chip(d) not in chips:
                chips.append(topo.chip(d))
        return sorted(chips, key=lambda ch: (ch != last_chip, -ch))

    def deliver(stage, via, j, dsts):
        for ch in chips_of(dsts):
            grp = [d for d in dsts if topo.chip(d) == ch]
            if ch != topo.chip(via) and len(grp) > 1:
                hops.append([stage, via, j, grp[:1]])
                hops.append([stage + 1, grp[0], j, grp[1:]])
            else:
                hops.append([stage, via, j, grp])

    gates, busy = {}, []
    for j, s in enumerate(cores):
        reach = [d for d in cores[j + 1:] if topo.may_write(s, d)]
        rest = [d for d in cores[j + 1:] if not topo.may_write(s, d)]
        if rest:
            gates[j] = [c for c in reach if all(topo.may_write(c, d) for d in rest)][0]
            if len(chips_of(rest)) > 1:
                busy.append(gates[j])
    for j, s in enumerate(cores):
        reach = [d for d in cores[j + 1:] if topo.may_write(s, d)]
        rest = [d for d in cores[j + 1:] if not topo.may_write(s, d)]
        gate = gates.get(j)
        if rest:
            hops.append([0, s, j, [gate]])
        away = [d for d in reach if d != gate and topo.chip(d) != topo.chip(s)]
        home = [d for d in reach if d != gate and topo.chip(d) == topo.chip(s)]
        if s in busy and len(away) > 1:
            deliver(0, s, j, away[:1])
            deliver(3, s, j, away[1:])
        elif away:
            deliver(0, s, j, away)
        if home:
            hops.append([0, s, j, home])
        if rest:
            deliver(1, gate, j, rest)
    return sorted(hops, key=lambda h: h[0])


def _mask(topo, src, dsts):
    m = topo.mask(src, dsts[0])
    for d in dsts[1:]:
        m &= topo.mask(src, d)
    return m, sum((m >> b) & 1 for b in range(m.bit_length()))


def rank_program(g, core, T, topo):
    cores = [int(c) for c in T.cores]
    S = T.sem
    hops = _plan(cores, topo)
    mine = [h for h in hops if h[1] == core]
    inbound = [h for h in hops if core in h[3]]
    rank = T.rank_of(core)
    if rank is None and not mine and not inbound:
        return

    def cols(t, j):
        return t[:, NC * j:NC * j + NC]

    def here(t, kind):
        if rank is not None and t == rank:
            return ("qh", 1)
        for (_, src, j, dsts) in inbound:
            if j == t:
                return ("%s%d" % (kind, j), _mask(topo, src, dsts)[1])
        return None

    stores = 0
    if rank is not None:
        v, pe, sc, sy = g.vector, g.tensor, g.scalar, g.sync
        sy.dma_start(T.xb[:], T.x[:]).then_inc(S.lx, 16)
        first = {}
        t0 = 0
        for n, w in enumerate(SPLIT):
            q = sc if n % 2 == 0 else sy
            q.dma_start(T.w1b[:, 512 * t0:512 * (t0 + w)], T.w1[:, 512 * t0:512 * (t0 + w)]).then_inc(S["lw%d" % n], 16)
            first[t0] = "lw%d" % n
            t0 += w
        sy.dma_start(T.w2b[:], T.w2[:]).then_inc(S.lv, 16)

        v.wait_ge(S.lx, 16)
        v.quantize_mx(T.xq[:], T.xs[:], T.xb[:]).then_inc(S.qx, 1)
        pe.wait_ge(S.qx, 1)
        for i in range(G):
            if i in first:
                v.wait_ge(S[first[i]], 16)
            v.quantize_mx(T.w1q[:, 128 * i:128 * i + 128], T.w1s[:, 128 * i:128 * i + 128],
                          T.w1b[:, 512 * i:512 * i + 512]).then_inc(S["qw%d" % i], 1)
            pe.wait_ge(S["qw%d" % i], 1)
            pe.matmul_mx(T.ps[:, BANK * i:BANK * i + NC], T.w1q[:, 128 * i:128 * i + 128],
                         T.w1s[:, 128 * i:128 * i + 128], T.xq[:], T.xs[:], True, True).then_inc(S["m%d" % i], 1)
        for i in range(G - 1):
            sc.wait_ge(S["m%d" % i], 1)
            sc.activation(T.hb[:, i:4 * NC:4], T.ps[:, BANK * i:BANK * i + NC], ActivationFunctionType.Relu,
                          scale=C).then_inc(S.acs, 1)
        i = G - 1
        v.wait_ge(S["m%d" % i], 1)
        v.tensor_scalar(T.hb[:, i:4 * NC:4], T.ps[:, BANK * i:BANK * i + NC], 0.0, C,
                        AluOpType.max, AluOpType.mult).then_inc(S.acv, 1)
        v.wait_ge(S.acs, G - 1)
        v.wait_ge(S.acv, 1)
        v.quantize_mx(cols(T.hq, rank), cols(T.hs, rank), T.hb[:]).then_inc(S.qh, 1)
        v.wait_ge(S.lv, 16)
        v.quantize_mx(T.w2q[:], T.w2s[:], T.w2b[:]).then_inc(S.qv, 1)

        order = sorted(inbound, key=lambda h: (h[0], [x for x in hops if x[1] == h[1]].index(h), hops.index(h)))
        units = [rank] + [h[2] for h in order]
        pe.wait_ge(S.qv, 1)
        for k, j in enumerate(units):
            for w in sorted(set(here(j, kind) for kind in "cs")):
                pe.wait_ge(S[w[0]], w[1])
            if k >= 4:
                pe.wait_ge(S["cp%d" % (k - 4)], 1)
            b = BANK * (4 + k % 4)
            z = T.ps[:, b:b + NC]
            pe.matmul_mx(z, T.w2q[:], T.w2s[:], cols(T.hq, j), cols(T.hs, j), True, True).then_inc(S["y%d" % k], 1)
            v.wait_ge(S["y%d" % k], 1)
            v.tensor_copy(cols(T.yb, j), z).then_inc(S["cp%d" % k], 1)
            sy.wait_ge(S["cp%d" % k], 1)
            sy.dma_start(cols(T.y, j), cols(T.yb, j)).then_inc(S["st%d" % k], 16)
        stores = len(units)

    sent = 0
    waited = []
    for (_, src, j, dsts) in mine:
        mask, n = _mask(topo, core, dsts)
        for kind in "cs":
            w = here(j, kind)
            if w not in waited:
                waited.append(w)
                g.wait_ge(S[w[0]], w[1])
            view = cols(T.hq, j).bitcast(dt.uint8) if kind == "c" else cols(T.hs, j)
            sem = S["%s%d" % (kind, j)]
            ids = [topo.addr(d) for d in dsts]
            if len(dsts) == 1:
                g.remote_dma(out_ap=view, in_ap=view, remote_sem=sem, local_sem=S.sent, pid=ids[0][1],
                             routing_id=ids[0][0], dma_engine_mask=mask)
            else:
                g.remote_dma_fused([RemoteDMATransfer(dst_ids=[DstId(rid=r, pnc=p) for (r, p, _) in ids],
                                                      dma_engine_mask=mask, remote_sem=sem, srcs=[view],
                                                      dsts=[view for _ in dsts])], local_sem=S.sent)
            sent += n
    if sent:
        g.wait_ge(S.sent, sent)
    for k in range(stores):
        g.wait_ge(S["st%d" % k], 16)
